import numpy as np
CORES = [5,13,21,29,37,45,53,61,69,77,85,93,101,109,117,125]
N = 16
def setup_inputs(rng):
    return {"x": rng.standard_normal((N, 128, 256), dtype=np.float32)}
def reference(x):
    s = x.sum(axis=0, dtype=np.float64).astype(x.dtype)
    return {"y": np.broadcast_to(s, (N,) + s.shape)}

@@ -1,0 +1,80 @@
+from concourse.bass import DstId, RemoteDMATransfer
+
+NP = 32
+PW = 8
+
+SCRATCH = {
+    "xs": ("dram", [NP, 128, PW], "float32"),
+    "out": ("dram", [NP, 128, PW], "float32"),
+    "hx": ("dram", [16, 128, PW], "float32"),
+    "mx": ("dram", [8, 128, PW], "float32"),
+    "rs": ("dram", [8, 128, PW], "float32"),
+    "ag": ("dram", [8, 128, PW], "float32"),
+}
+SEMAPHORES = ["ld", "st", "s1", "s2", "s3", "s4", "s5", "sent"]
+
+HELPER = {0: 6, 1: 2}
+
+
+def rank_program(g, core, T, topo):
+    c, k = topo.chip(core), core % 8
+    p = c & 1
+    S = T.sem
+
+    def dst(cr):
+        rid, pid, _se = topo.addr(cr)
+        return DstId(rid=rid, pnc=pid)
+
+    def helper(ch, d):
+        return ch * 8 + HELPER[d]
+
+    def rank_core(ch):
+        return T.cores[ch]
+
+    if T.rank_of(core) is not None:
+        g.dma_start(T.xs[:], T.x[:]).then_inc(S.ld, 16)
+        g.wait_ge(S.ld, 16)
+        for d in (0, 1):
+            g.remote_dma_fused(
+                [RemoteDMATransfer(dst_ids=[dst(helper(c, d))], dma_engine_mask=1 << o, remote_sem=S.s1,
+                                   src=T.xs[16 * d + o], dst=T.hx[o]) for o in range(16)],
+                local_sem=S.sent)
+        g.wait_ge(S.sent, 32)
+        g.wait_ge(S.s4, 4 * 8)
+        g.wait_ge(S.s5, 4 * 7)
+        g.dma_start(T.y[:], T.out[:]).then_inc(S.st, 16)
+        g.wait_ge(S.st, 16)
+        return
+
+    if k not in (HELPER[0], HELPER[1]):
+        return
+
+    d = topo.die(core)
+    others = [j for j in range(p, 16, 2) if j != c]
+    g.wait_ge(S.s1, 16)
+    g.remote_dma_fused(
+        [RemoteDMATransfer(dst_ids=[dst(helper(c ^ 1, d))], dma_engine_mask=1 << i, remote_sem=S.s2,
+                           src=T.hx[2 * i + (1 - p)], dst=T.mx[i]) for i in range(8)],
+        local_sem=S.sent)
+    g.wait_ge(S.s2, 8)
+    g.remote_dma_fused(
+        [RemoteDMATransfer(dst_ids=[dst(helper(j, d))], dma_engine_mask=1 << i, remote_sem=S.s3,
+                           srcs=[T.hx[j], T.mx[j // 2]], dsts=[T.rs[c // 2]], alu_op=1)
+         for i, j in enumerate(others)],
+        local_sem=S.sent)
+    g.wait_ge(S.s3, 7)
+    q = 16 * d + c
+    g.remote_dma_fused(
+        [RemoteDMATransfer(
+            dst_ids=[dst(helper(j, d)) for j in others] + [dst(rank_core(c)), dst(rank_core(c ^ 1))],
+            dma_engine_mask=0xFF, remote_sem=S.s4,
+            srcs=[T.hx[c], T.mx[c // 2]] + [T.rs[j // 2] for j in others],
+            dsts=[T.ag[c // 2] for j in others] + [T.out[q], T.out[q]], alu_op=1)],
+        local_sem=S.sent)
+    g.wait_ge(S.s4, 7 * 8)
+    g.remote_dma_fused(
+        [RemoteDMATransfer(dst_ids=[dst(rank_core(c)), dst(rank_core(c ^ 1))], dma_engine_mask=1 << i,
+                           remote_sem=S.s5, srcs=[T.ag[j // 2]], dsts=[T.out[16 * d + j], T.out[16 * d + j]])
+         for i, j in enumerate(others)],
+        local_sem=S.sent)
+    g.wait_ge(S.sent, 8 + 7 + 8 + 7)

@@ -1,80 +1,60 @@
 from concourse.bass import DstId, RemoteDMATransfer
 
-NP = 32
-PW = 8
+PW = 16
 
 SCRATCH = {
-    "xs": ("dram", [NP, 128, PW], "float32"),
-    "out": ("dram", [NP, 128, PW], "float32"),
-    "hx": ("dram", [16, 128, PW], "float32"),
-    "mx": ("dram", [8, 128, PW], "float32"),
+    "xs": ("dram", [16, 128, PW], "float32"),
+    "out": ("dram", [16, 128, PW], "float32"),
     "rs": ("dram", [8, 128, PW], "float32"),
-    "ag": ("dram", [8, 128, PW], "float32"),
+    "mp": ("dram", [128, PW], "float32"),
 }
-SEMAPHORES = ["ld", "st", "s1", "s2", "s3", "s4", "s5", "sent"]
+SEMAPHORES = ["ld0", "ld1", "s1", "s2", "fin0", "fin1", "st0", "st1", "sent"]
 
-HELPER = {0: 6, 1: 2}
+HELPERS = (2, 3)
 
 
 def rank_program(g, core, T, topo):
     c, k = topo.chip(core), core % 8
-    p = c & 1
     S = T.sem
+    plane = list(range(c & 1, 16, 2))
 
     def dst(cr):
         rid, pid, _se = topo.addr(cr)
         return DstId(rid=rid, pnc=pid)
 
-    def helper(ch, d):
-        return ch * 8 + HELPER[d]
-
-    def rank_core(ch):
-        return T.cores[ch]
-
     if T.rank_of(core) is not None:
-        g.dma_start(T.xs[:], T.x[:]).then_inc(S.ld, 16)
-        g.wait_ge(S.ld, 16)
-        for d in (0, 1):
+        queues = (g.sync, g.scalar)
+        for h in (0, 1):
+            queues[h].dma_start(T.xs[8 * h:8 * h + 8], T.x[64 * h:64 * h + 64, :]).then_inc(S["ld%d" % h], 16)
+        for h in (0, 1):
+            g.wait_ge(S["ld%d" % h], 16)
             g.remote_dma_fused(
-                [RemoteDMATransfer(dst_ids=[dst(helper(c, d))], dma_engine_mask=1 << o, remote_sem=S.s1,
-                                   src=T.xs[16 * d + o], dst=T.hx[o]) for o in range(16)],
+                [RemoteDMATransfer(dst_ids=[dst(j * 8 + HELPERS[h])], dma_engine_mask=1 << (j // 2), remote_sem=S.s1,
+                                   src=T.xs[8 * h + j // 2], dst=T.rs[c // 2]) for j in plane],
                 local_sem=S.sent)
-        g.wait_ge(S.sent, 32)
-        g.wait_ge(S.s4, 4 * 8)
-        g.wait_ge(S.s5, 4 * 7)
-        g.dma_start(T.y[:], T.out[:]).then_inc(S.st, 16)
-        g.wait_ge(S.st, 16)
+        for h in (0, 1):
+            queues[h].wait_ge(S["fin%d" % h], 8 * 8)
+            queues[h].dma_start(T.y[64 * h:64 * h + 64, :], T.out[8 * h:8 * h + 8]).then_inc(S["st%d" % h], 16)
+        g.wait_ge(S.sent, 16)
+        g.wait_ge(S.st0, 16)
+        g.wait_ge(S.st1, 16)
         return
 
-    if k not in (HELPER[0], HELPER[1]):
+    if k not in HELPERS:
         return
 
-    d = topo.die(core)
-    others = [j for j in range(p, 16, 2) if j != c]
-    g.wait_ge(S.s1, 16)
+    h = HELPERS.index(k)
+    mine = [T.rs[i] for i in range(8)]
+    g.wait_ge(S.s1, 8)
     g.remote_dma_fused(
-        [RemoteDMATransfer(dst_ids=[dst(helper(c ^ 1, d))], dma_engine_mask=1 << i, remote_sem=S.s2,
-                           src=T.hx[2 * i + (1 - p)], dst=T.mx[i]) for i in range(8)],
+        [RemoteDMATransfer(dst_ids=[dst((c ^ 1) * 8 + k)], dma_engine_mask=0xFF, remote_sem=S.s2,
+                           srcs=mine, dsts=[T.mp[:]], alu_op=1)],
         local_sem=S.sent)
     g.wait_ge(S.s2, 8)
+    q = 8 * h + c // 2
     g.remote_dma_fused(
-        [RemoteDMATransfer(dst_ids=[dst(helper(j, d))], dma_engine_mask=1 << i, remote_sem=S.s3,
-                           srcs=[T.hx[j], T.mx[j // 2]], dsts=[T.rs[c // 2]], alu_op=1)
-         for i, j in enumerate(others)],
+        [RemoteDMATransfer(dst_ids=[dst(T.cores[j]) for j in plane], dma_engine_mask=0xFF,
+                           remote_sem=S["fin%d" % h], srcs=mine + [T.mp[:]], dsts=[T.out[q] for j in plane],
+                           alu_op=1)],
         local_sem=S.sent)
-    g.wait_ge(S.s3, 7)
-    q = 16 * d + c
-    g.remote_dma_fused(
-        [RemoteDMATransfer(
-            dst_ids=[dst(helper(j, d)) for j in others] + [dst(rank_core(c)), dst(rank_core(c ^ 1))],
-            dma_engine_mask=0xFF, remote_sem=S.s4,
-            srcs=[T.hx[c], T.mx[c // 2]] + [T.rs[j // 2] for j in others],
-            dsts=[T.ag[c // 2] for j in others] + [T.out[q], T.out[q]], alu_op=1)],
-        local_sem=S.sent)
-    g.wait_ge(S.s4, 7 * 8)
-    g.remote_dma_fused(
-        [RemoteDMATransfer(dst_ids=[dst(rank_core(c)), dst(rank_core(c ^ 1))], dma_engine_mask=1 << i,
-                           remote_sem=S.s5, srcs=[T.ag[j // 2]], dsts=[T.out[16 * d + j], T.out[16 * d + j]])
-         for i, j in enumerate(others)],
-        local_sem=S.sent)
-    g.wait_ge(S.sent, 8 + 7 + 8 + 7)
+    g.wait_ge(S.sent, 16)

from concourse.bass import DstId, RemoteDMATransfer

PW = 16

SCRATCH = {
    "xs": ("dram", [16, 128, PW], "float32"),
    "out": ("dram", [16, 128, PW], "float32"),
    "rs": ("dram", [8, 128, PW], "float32"),
    "mp": ("dram", [128, PW], "float32"),
}
SEMAPHORES = ["ld0", "ld1", "s1", "s2", "fin0", "fin1", "st0", "st1", "sent"]

HELPERS = (2, 3)


def rank_program(g, core, T, topo):
    c, k = topo.chip(core), core % 8
    S = T.sem
    plane = list(range(c & 1, 16, 2))

    def dst(cr):
        rid, pid, _se = topo.addr(cr)
        return DstId(rid=rid, pnc=pid)

    if T.rank_of(core) is not None:
        queues = (g.sync, g.scalar)
        for h in (0, 1):
            queues[h].dma_start(T.xs[8 * h:8 * h + 8], T.x[64 * h:64 * h + 64, :]).then_inc(S["ld%d" % h], 16)
        for h in (0, 1):
            g.wait_ge(S["ld%d" % h], 16)
            g.remote_dma_fused(
                [RemoteDMATransfer(dst_ids=[dst(j * 8 + HELPERS[h])], dma_engine_mask=1 << (j // 2), remote_sem=S.s1,
                                   src=T.xs[8 * h + j // 2], dst=T.rs[c // 2]) for j in plane],
                local_sem=S.sent)
        for h in (0, 1):
            queues[h].wait_ge(S["fin%d" % h], 8 * 8)
            queues[h].dma_start(T.y[64 * h:64 * h + 64, :], T.out[8 * h:8 * h + 8]).then_inc(S["st%d" % h], 16)
        g.wait_ge(S.sent, 16)
        g.wait_ge(S.st0, 16)
        g.wait_ge(S.st1, 16)
        return

    if k not in HELPERS:
        return

    h = HELPERS.index(k)
    mine = [T.rs[i] for i in range(8)]
    g.wait_ge(S.s1, 8)
    g.remote_dma_fused(
        [RemoteDMATransfer(dst_ids=[dst((c ^ 1) * 8 + k)], dma_engine_mask=0xFF, remote_sem=S.s2,
                           srcs=mine, dsts=[T.mp[:]], alu_op=1)],
        local_sem=S.sent)
    g.wait_ge(S.s2, 8)
    q = 8 * h + c // 2
    g.remote_dma_fused(
        [RemoteDMATransfer(dst_ids=[dst(T.cores[j]) for j in plane], dma_engine_mask=0xFF,
                           remote_sem=S["fin%d" % h], srcs=mine + [T.mp[:]], dsts=[T.out[q] for j in plane],
                           alu_op=1)],
        local_sem=S.sent)
    g.wait_ge(S.sent, 16)
